import numpy as np, ml_dtypes
CORES = [2,6,10,14,18,22,26,30]
N = 8
BF = ml_dtypes.bfloat16
def f(rng, *shape):
    return (rng.standard_normal(shape, dtype=np.float32) * np.exp2(rng.integers(-2, 3, shape[:-1] + (1,)))).astype(BF)
def wide(rng, *shape):
    v = f(rng, *shape).astype(np.float32); k = shape[:-2] + (1, shape[-1])
    return (v * np.exp2(rng.integers(-6, 7, k)) * (rng.random(k) > 0.0625)).astype(BF)
P, NT, W, D = 1024, 128, 512, 64
def order(g):
    return range(N)
def places(ln):
    n = np.asarray(ln).reshape(-1, NT).astype(np.int64) + 1; m = len(n)
    t = np.repeat(np.tile(np.arange(NT), m), n.reshape(-1)).reshape(m, P)
    last = np.zeros((m, P), bool); last[np.arange(m)[:, None], np.add.accumulate(n, 1) - 1] = True
    return t, last
def steps(ln, ds):
    t, last = places(ln); m = len(t); src = np.arange(P) - np.take_along_axis(np.asarray(ds).reshape(m, NT).astype(np.int64), t, 1)
    e = np.zeros((m, P), np.int64); row = np.arange(m)
    for i in range(P):
        j = src[:, i]; e[:, i] = np.where(last[:, i], 0, 1 + np.where(j >= 0, e[row, np.maximum(j, 0)], 0))
    return e
def lengths(rng, at, big):
    n = np.zeros((N, 8, NT), np.int64)
    for r in range(N):
        for g in range(8):
            b = int(big[r, g]); rest = P - NT - b
            v = np.minimum(rng.multinomial(rest, rng.dirichlet(np.where(rng.random(NT - 1) < 0.25, 0.001, 1.0))), D)
            v = v + rng.multivariate_hypergeometric(D - v, rest - int(np.sum(v)))
            n[r, g] = np.insert(v, int(at[r, g]), b)
    return n
def starts(n):
    return np.add.accumulate(n + 1, 2) - n - 1
def distances(rng, n):
    s = starts(n); k = rng.integers(0, 4, n.shape)
    over = rng.integers(np.minimum(s, W - 1) + 1, W + 1)
    return np.where(k == 0, rng.integers(1, 9, n.shape), np.where(k == 3, over, rng.integers(1, W + 1, n.shape)))
def inside(rng, n, d, share):
    s = starts(n); d = np.array(d)
    for g in range(8):
        q = order(g)[0]; m = (d[q, g] > s[q, g]) & (s[q, g] > 0) & (rng.random(NT) < share)
        d[q, g] = np.where(m, rng.integers(1, np.maximum(s[q, g], 1) + 1), d[q, g])
    return d
def fit(n, d):
    d = np.array(d)
    for r in range(N):
        for g in range(8):
            e = []
            for t, (c, k) in enumerate(zip(n[r, g].tolist(), d[r, g].tolist())):
                s = len(e)
                for i in range(s, s + c): e.append(1 + (e[i - k] if i >= k else 0))
                if max(e[s:], default=0) > D:
                    d[r, g, t] = 1; e[s:] = range(1, c + 1)
                e.append(0)
    return d
def pack(rng, n, d):
    return {"ln": n.astype(np.int32), "ds": d.astype(np.int32), "le": f(rng, N, 128, NT)}
def setup_inputs(rng):
    n = lengths(rng, rng.integers(0, NT, (N, 8)), rng.integers(1, D + 1, (N, 8)))
    return pack(rng, n, fit(n, inside(rng, n, distances(rng, n), 0.75)))
def setup_inputs_deep(rng):
    at = np.where(rng.random((N, 8)) < 0.25, rng.choice(np.array([0, NT - 1]), (N, 8)), rng.integers(0, NT, (N, 8)))
    n = lengths(rng, at, np.full((N, 8), D)); d = np.where(rng.random(n.shape) < 0.5, rng.integers(1, 4, n.shape), distances(rng, n))
    d = inside(rng, n, d, 0.75); np.put_along_axis(d, at[:, :, None], 1, 2)
    return pack(rng, n, fit(n, d))
def setup_inputs_hops(rng):
    n = lengths(rng, rng.integers(0, NT, (N, 8)), rng.integers(1, D + 1, (N, 8)))
    return pack(rng, n, fit(n, inside(rng, n, rng.integers(W - 8, W + 1, n.shape), 1.0)))
def setup_inputs_ends(rng):
    at = rng.choice(np.array([0, NT - 1]), (N, 8)); at[:, :2] = 0
    n = lengths(rng, at, rng.integers(2, D + 1, (N, 8))); n[rng.integers(0, N)] = P // NT - 1
    s = starts(n); d = np.choose(rng.integers(0, 6, n.shape), [s * 0 + W, s * 0 + 1, s, s + 1, s + n, n])
    d = inside(rng, n, np.minimum(np.maximum(d, 1), W), 0.5); d[:, 0, 0] = W; d[:, 1, 0] = 1
    return pack(rng, n, fit(n, d))
def setup_inputs_long(rng):
    at = rng.integers(0, NT, (N, 8)); k = rng.integers(P // D, W + 1, (N, 8)); u = rng.integers(0, 3, (N, 8)); k = np.where(u == 0, P // D, np.where(u == 1, W, k))
    for g in range(8):
        q = order(g)[0]; at[q, g] = NT - 1; k[q, g] = rng.integers(P // D, min(W, NT - 1) + 1)
    n = np.zeros((N, 8, NT), np.int64); np.put_along_axis(n, at[:, :, None], P - NT, 2)
    d = rng.integers(1, W + 1, n.shape); np.put_along_axis(d, at[:, :, None], k[:, :, None], 2)
    return pack(rng, n, d)
def setup_inputs_spread(rng):
    d = setup_inputs(rng); d["le"] = wide(rng, N, 128, NT); return d
def check_inputs(d):
    bad = []; a = np.asarray(d["ln"]).astype(np.int64); b = np.asarray(d["ds"]).astype(np.int64)
    if (a < 0).any() or (np.sum(a, 2) + NT != P).any(): bad.append("lengths")
    if (b < 1).any() or (b > W).any(): bad.append("distances")
    if not bad and (steps(a, b) > D).any(): bad.append("steps")
    if not np.isfinite(np.asarray(d["le"]).astype(np.float32)).all(): bad.append("finite")
    return bad
def reference(ln, ds, le):
    y = np.zeros((N, 128, P), BF); t, last = places(ln); t = t.reshape(N, 8, P); last = last.reshape(N, 8, P)
    for g in range(8):
        buf = np.zeros((W + P, 16), BF)
        for r in order(g):
            a = np.ascontiguousarray(le[r, 16 * g:16 * g + 16].T); k = ds[r, g][t[r, g]].tolist(); tk = t[r, g].tolist(); own = last[r, g].tolist()
            for i in range(P):
                buf[W + i] = a[tk[i]] if own[i] else buf[W + i - k[i]]
            y[r, 16 * g:16 * g + 16] = buf[W:].T
            buf[:W] = buf[P:]
    return {"y": y}

@@ -1,0 +1,270 @@
+from concourse.bass import DstId, RemoteDMATransfer
+from concourse.mybir import AluOpType, ActivationFunctionType
+
+P, NT, W = 1024, 128, 512
+NL = NT + W
+NC = NL + P
+OFF = 2064.0
+KB = OFF - 7.5
+
+SCRATCH = {
+    "lnI": ("sbuf", [128, 128], "int32"), "dsI": ("sbuf", [128, 128], "int32"),
+    "lnF": ("sbuf", [128, 128], "float16"), "dd": ("sbuf", [128, 128], "float16"),
+    "pI": ("sbuf", [128, 8], "int32"), "rtI": ("sbuf", [128, 8], "int32"), "qgI": ("sbuf", [128, 8], "int32"),
+    "rt": ("sbuf", [128, 8], "float32"), "qg": ("sbuf", [128, 8], "float32"),
+    "kb": ("sbuf", [128, 8], "float32"), "kc": ("sbuf", [128, 8], "float32"),
+    "selV": ("sbuf", [128, 128], "float32"), "Sel": ("sbuf", [128, 128], "float16"),
+    "rV": ("sbuf", [128, 128], "float32"), "mask": ("sbuf", [128, 256], "bfloat16"),
+    "bV": ("sbuf", [128, 8], "float32"), "B": ("sbuf", [128, 16], "float16"),
+    "qV": ("sbuf", [128, 144], "float32"), "Q": ("sbuf", [128, 144], "bfloat16"),
+    "mV": ("sbuf", [128, NL], "float32"),
+    "Z": ("sbuf", [128, 1040], "float32"), "Zv": ("sbuf", [128, 128], "float32"), "ini": ("sbuf", [128, 8], "float32"),
+    "AA": ("sbuf", [128, 256], "float16"), "offs": ("sbuf", [128, 8], "uint16"),
+    "T0": ("sbuf", [128, NC], "bfloat16"), "T1": ("sbuf", [128, NC], "bfloat16"), "T2": ("sbuf", [128, NC], "bfloat16"),
+    "L0": ("sbuf", [128, 64], "uint16"), "L1": ("sbuf", [128, 64], "uint16"), "L2": ("sbuf", [128, 64], "uint16"),
+    "LF": ("sbuf", [128, 64], "uint16"),
+    "M": ("sbuf", [128, 256], "uint16"),
+    "D": ("sbuf", [128, 8 * NL], "bfloat16"),
+    "Y": ("sbuf", [128, P], "bfloat16"),
+    "psA": ("psum", [128, 512], "float32"), "psE": ("psum", [128, 512], "float32"), "psD": ("psum", [128, 512], "float32"),
+    "psW0": ("psum", [128, 512], "float32"), "psW1": ("psum", [128, 512], "float32"), "psW2": ("psum", [128, 512], "float32"),
+}
+SEMAPHORES = ["qv", "qa", "qp", "qg", "ldln", "ldds", "ldle", "st0", "st1", "lea", "sent"] + ["m%d" % s for s in range(8)]
+
+
+def rank_program(g, core, T, topo):
+    rank = T.rank_of(core)
+    if rank is None:
+        return
+    queue = {"v": g.vector, "a": g.scalar, "p": g.tensor, "g": g, "s": g.sync}
+    known = {e: {} for e in queue}
+    snap = {}
+    count = {}
+    acc = {}
+
+    def await_tokens(e, toks):
+        best = {}
+        for s, v in toks:
+            if known[e].get(s, 0) < v:
+                best[s] = max(best.get(s, 0), v)
+        for s, v in sorted(best.items()):
+            if any(t != s and snap.get((t, best[t]), {}).get(s, 0) >= v for t in best):
+                continue
+            if known[e].get(s, 0) >= v:
+                continue
+            queue[e].wait_ge(T.sem[s], v)
+            known[e][s] = v
+            for t, w in snap.get((s, v), {}).items():
+                known[e][t] = max(known[e].get(t, 0), w)
+
+    def depend(e, reads, writes):
+        toks = []
+        for b, lo, hi in reads:
+            toks += [a[3] for a in acc.get(b, []) if a[2] and a[0] < hi and lo < a[1]]
+        for b, lo, hi in writes:
+            toks += [a[3] for a in acc.get(b, []) if a[0] < hi and lo < a[1]]
+        await_tokens(e, toks)
+
+    def record(e, tok, reads, writes):
+        if e is not None:
+            snap[tok] = dict(known[e])
+            snap[tok][tok[0]] = tok[1]
+        for b, lo, hi in writes:
+            acc[b] = [a for a in acc.get(b, []) if not (lo <= a[0] and a[1] <= hi)] + [[lo, hi, True, tok]]
+        for b, lo, hi in reads:
+            acc.setdefault(b, []).append([lo, hi, False, tok])
+
+    def op(e, call, reads, writes):
+        depend(e, reads, writes)
+        s = "q" + e
+        count[s] = count.get(s, 0) + 1
+        call(queue[e]).then_inc(T.sem[s], 1)
+        record(e, (s, count[s]), reads, writes)
+
+    def dma(e, sem, out, in_, reads, writes):
+        depend(e, reads, writes)
+        count[sem] = count.get(sem, 0) + 16
+        queue[e].dma_start(out, in_).then_inc(T.sem[sem], 16)
+        record(e, (sem, count[sem]), reads, writes)
+
+    later = [c for c in T.cores if T.rank_of(c) > rank]
+    sent = [0]
+
+    def lanes(src, dst):
+        if topo.chip(src) != topo.chip(dst):
+            return topo.engines(src, dst)
+        off = [x for c in T.cores if topo.chip(c) != topo.chip(src) and T.rank_of(c) > T.rank_of(src)
+               for x in topo.engines(src, c)]
+        return [x for x in topo.engines(src, dst) if x not in off]
+
+    def send(cores, name, lo, hi, sem, dst_name, dlo, dhi):
+        if not cores:
+            return
+        depend("g", [(name, lo, hi)], [])
+        sets = []
+        for c in cores:
+            e = lanes(core, c)
+            same = [x for x in sets if x[0] == e]
+            if same:
+                same[0][1].append(c)
+            else:
+                sets.append([e, [c]])
+        trs = []
+        for e, cs in sets:
+            ids = []
+            for c in cs:
+                rid, pid, _ = topo.addr(c)
+                ids.append(DstId(rid=rid, pnc=pid))
+            trs.append(RemoteDMATransfer(dst_ids=ids, dma_engine_mask=sum(1 << x for x in e), remote_sem=T.sem[sem],
+                                         srcs=[T[name][:, lo:hi]], dsts=[T[dst_name][:, dlo:dhi] for _ in cs]))
+            sent[0] += len(e)
+        g.remote_dma_fused(trs, local_sem=T.sem.sent)
+
+    A, F = AluOpType, ActivationFunctionType
+
+    if rank:
+        record(None, ("lea", sum(len(lanes(T.cores[s], core)) for s in range(rank))), [],
+               [("D", NL * s, NL * s + NT) for s in range(rank)])
+        for s in range(rank):
+            record(None, ("m%d" % s, len(lanes(T.cores[s], core))), [], [("M", 32 * s, 32 * s + 32)])
+
+    dma("s", "ldln", T.lnI[0:8, :], T.ln[:], [], [("lnI", 0, 128)])
+    dma("a", "ldds", T.dsI[0:8, :], T.ds[:], [], [("dsI", 0, 128)])
+    dma("s", "ldle", T.D[:, NL * rank:NL * rank + NT], T.le[:], [], [("D", NL * rank, NL * rank + NT)])
+
+    def iota(name, rows, n, pattern, base, cm):
+        out = T[name][0:rows, 0:n]
+        if name == "pI":
+            op("g", lambda q: q.iota(out, pattern, base, cm), [], [(name, 0, n)])
+        else:
+            op("g", lambda q: q.iota(out, pattern, base, cm, allow_small_or_imprecise_dtypes=True), [], [(name, 0, n)])
+
+    iota("pI", 128, 1, [[1, 1]], 0, 1)
+    iota("selV", 8, 128, [[1, 8], [0, 16]], 0, -1)
+    iota("rV", 128, 128, [[0, 8], [1, 16]], 0, 0)
+    iota("bV", 128, 8, [[1, 8]], 0, 0)
+    iota("qV", 128, 144, [[1, 9], [1000, 16]], -1, 0)
+    iota("mV", 128, NL, [[1, NL]], 0, 0)
+
+    def vs(out, in0, s1, s2, op0, op1, reads, writes):
+        if op1 is None:
+            op("v", lambda q: q.tensor_scalar(out, in0, s1, None, op0), reads, writes)
+        else:
+            op("v", lambda q: q.tensor_scalar(out, in0, s1, s2, op0, op1), reads, writes)
+
+    def fill(name, lo, hi, c):
+        op("v", lambda q: q.memset(T[name][:, lo:hi], c), [], [(name, lo, hi)])
+
+    fill("mask", 0, 128, 1.0)
+    vs(T.rtI[:, 0:1], T.pI[:, 0:1], 15, None, A.bitwise_and, None, [("pI", 0, 1)], [("rtI", 0, 1)])
+    vs(T.qgI[:, 0:1], T.pI[:, 0:1], 4, None, A.arith_shift_right, None, [("pI", 0, 1)], [("qgI", 0, 1)])
+    vs(T.Sel[0:8, :], T.selV[0:8, :], 0.0, None, A.is_equal, None, [("selV", 0, 128)], [("Sel", 0, 128)])
+    op("v", lambda q: q.tensor_copy(T.rt[:, 0:1], T.rtI[:, 0:1]), [("rtI", 0, 1)], [("rt", 0, 1)])
+    op("v", lambda q: q.tensor_copy(T.qg[:, 0:1], T.qgI[:, 0:1]), [("qgI", 0, 1)], [("qg", 0, 1)])
+    vs(T.kc[:, 0:1], T.rtI[:, 0:1], KB + NL - 1, None, A.add, None, [("rtI", 0, 1)], [("kc", 0, 1)])
+    vs(T.kb[:, 0:1], T.rtI[:, 0:1], KB, None, A.add, None, [("rtI", 0, 1)], [("kb", 0, 1)])
+    vs(T.mask[:, 128:256], T.rV[:], T.rt[:, 0:1], None, A.is_ge, None, [("rV", 0, 128), ("rt", 0, 1)], [("mask", 128, 256)])
+    vs(T.B[:, 0:8], T.bV[:], T.qg[:, 0:1], None, A.is_gt, None, [("bV", 0, 8), ("qg", 0, 1)], [("B", 0, 8)])
+    vs(T.B[:, 8:16], T.bV[:], T.qg[:, 0:1], None, A.is_equal, None, [("bV", 0, 8), ("qg", 0, 1)], [("B", 8, 16)])
+    fill("Z", 0, 1040, 0.5)
+
+    vs(T.lnF[0:8, :], T.lnI[0:8, :], 1.0, None, A.add, None, [("lnI", 0, 128)], [("lnF", 0, 128)])
+
+    def mm_a(q):
+        q.matmul(T.psA[:, 0:128], T.lnF[0:8, :], T.Sel[0:8, :], True, True)
+        return q.matmul(T.psA[:, 128:256], T.lnF[0:8, :], T.Sel[0:8, :], True, True)
+    op("p", mm_a, [("lnF", 0, 128), ("Sel", 0, 128)], [("psA", 0, 512)])
+    op("v", lambda q: q.tensor_tensor(T.dd[0:8, 0:127], T.dsI[0:8, 0:127], T.dsI[0:8, 1:128], A.subtract),
+       [("dsI", 0, 128)], [("dd", 0, 127)])
+    op("v", lambda q: q.tensor_copy(T.dd[0:8, 127:128], T.dsI[0:8, 0:1]), [("dsI", 0, 128)], [("dd", 127, 128)])
+    op("p", lambda q: q.matmul(T.psD[:, 0:128], T.Sel[0:8, :], T.dd[0:8, :], True, True),
+       [("Sel", 0, 128), ("dd", 0, 128)], [("psD", 0, 512)])
+    op("v", lambda q: q.tensor_tensor(T.AA[:], T.psA[:, 0:256], T.mask[:], A.mult),
+       [("psA", 0, 512), ("mask", 0, 256)], [("AA", 0, 256)])
+
+    def mm_e(q):
+        q.matmul(T.psE[:, 0:8], T.AA[:, 0:128], T.B[:, 0:8], True, False)
+        return q.matmul(T.psE[:, 0:8], T.AA[:, 128:256], T.B[:, 8:16], False, True)
+    op("p", mm_e, [("AA", 0, 256), ("B", 0, 16)], [("psE", 0, 512)])
+    op("a", lambda q: q.activation(T.Zv[:], T.psD[:, 0:128], F.Copy, bias=0.5, scale=0.5), [("psD", 0, 512)], [("Zv", 0, 128)])
+    op("a", lambda q: q.activation(T.ini[:, 0:1], T.psD[:, 127:128], F.Identity, bias=T.kc[:, 0:1], scale=-1.0),
+       [("psD", 0, 512), ("kc", 0, 1)], [("ini", 0, 1)])
+    for b in range(3):
+        tab = T["T%d" % b]
+        op("a", lambda q: q.activation(tab[:, 0:NL], T.mV[:], F.Identity, bias=T.kb[:, 0:1]),
+           [("mV", 0, NL), ("kb", 0, 1)], [("T%d" % b, 0, NL)])
+    vs(T.Q[:], T.qV[:], T.qg[:, 0:1], 0.0625, A.is_equal, A.mult, [("qV", 0, 144), ("qg", 0, 1)], [("Q", 0, 144)])
+    vs(T.offs[:], T.psE[:, 0:8], -1.0, None, A.add, None, [("psE", 0, 512)], [("offs", 0, 8)])
+
+    op("v", lambda q: q.tensor_copy(T.Z[:, 8:8 + P].indirect(T.offs[:, 0:8]), T.Zv[:]),
+       [("Zv", 0, 128), ("offs", 0, 8)], [("Z", 8, 8 + P)])
+    op("v", lambda q: q.tensor_tensor_scan(T.T0[:, NL:NC], T.Z[:, 7:7 + P], T.Z[:, 7:7 + P], T.ini[:, 0:1], A.add, A.add),
+       [("Z", 0, 1040), ("ini", 0, 1)], [("T0", NL, NC)])
+    op("v", lambda q: q.tensor_copy(T.T0[:, NL:NC].indirect(T.offs[:, 0:8]), T.T0[:, 0:NT]),
+       [("T0", 0, NT), ("offs", 0, 8)], [("T0", NL, NC)])
+
+    send(later, "D", NL * rank, NL * rank + NT, "lea", "D", NL * rank, NL * rank + NT)
+
+    def bank(n, hi):
+        return "psW%d" % (n % 3 if hi == P else (n + 1) % 3)
+
+    def wrap(n, lo, hi):
+        tab, b = "T%d" % (n % 3), bank(n, hi)
+
+        def go(q):
+            for k in range(16):
+                last = q.matmul(T[b][:, 0:(hi - lo) // 16], T.Q[:, 16 - k:144 - k], T[tab][:, NL + lo + k:NL + hi:16], k == 0, k == 15)
+            return last
+        op("p", go, [("Q", 0, 144), (tab, NL + lo, NL + hi)], [(b, 0, 512)])
+
+    def to_list(n, name, lo, hi, c0):
+        b, w = bank(n, hi), (hi - lo) // 16
+        vs(T[name][:, c0:c0 + w], T[b][:, 0:w], -OFF, None, A.add, None, [(b, 0, 512)], [(name, c0, c0 + w)])
+
+    def gather(e, out, olo, win, wlo, whi, lst, c0, c1):
+        o, i = T[out][:, olo:olo + 16 * (c1 - c0)], T[win][:, wlo:whi].indirect(T[lst][:, c0:c1])
+        r, w = [(win, wlo, whi), (lst, c0, c1)], [(out, olo, olo + 16 * (c1 - c0))]
+        if e == "v":
+            op("v", lambda q: q.tensor_copy(o, i), r, w)
+        else:
+            op("a", lambda q: q.activation(o, i, F.Copy), r, w)
+
+    def compose(n, m, lo, hi):
+        new, old, lst = "T%d" % (n % 3), "T%d" % ((n - 1) % 3), "L%d" % (m % 3)
+        mid = (lo + hi) // 2
+        gather("v", new, NL + lo, old, 0, NC, lst, lo // 16, mid // 16)
+        gather("a", new, NL + mid, old, 0, NC, lst, mid // 16, hi // 16)
+
+    wrap(0, 0, P)
+    fill("D", NT, NL, 0.0)
+    to_list(0, "L0", 0, P, 0)
+    compose(1, 0, 0, P)
+    wrap(1, 0, P)
+    for n in range(2, 9):
+        compose(n, n - 2, 0, P)
+        to_list(n - 1, "L%d" % ((n - 1) % 3), 0, P, 0)
+        if n < 8:
+            wrap(n, 0, P)
+    compose(9, 7, W, P)
+    wrap(9, W, P)
+    compose(9, 7, 0, W)
+    wrap(9, 0, W)
+    to_list(9, "LF", W, P, 32)
+    order = sorted(later, key=lambda c: -T.rank_of(c))
+    for a, b in ((0, 2), (2, 4), (4, 7)):
+        send(order[a:b], "LF", 32, 64, "m%d" % rank, "M", 32 * rank, 32 * rank + 32)
+    to_list(9, "LF", 0, W, 0)
+
+    for s in range(rank):
+        gather("v", "D", NL * (s + 1) + NT, "D", NL * s, NL * s + NL, "M", 32 * s, 32 * s + 16)
+        gather("a", "D", NL * (s + 1) + NT + 256, "D", NL * s, NL * s + NL, "M", 32 * s + 16, 32 * s + 32)
+    gather("v", "Y", 0, "D", NL * rank, NL * rank + NL, "LF", 0, 32)
+    gather("a", "Y", W, "D", NL * rank, NL * rank + NL, "LF", 32, 64)
+    dma("s", "st0", T.y[:, 0:W], T.Y[:, 0:W], [("Y", 0, W)], [])
+    dma("a", "st1", T.y[:, W:P], T.Y[:, W:P], [("Y", W, P)], [])
+    for s in ("qv", "qa", "qp", "qg", "ldln", "ldds", "ldle"):
+        await_tokens("s", [(s, count[s])])
+    if sent[0]:
+        g.wait_ge(T.sem.sent, sent[0])
+    await_tokens("s", [("st0", 16)])
+    await_tokens("a", [("st1", 16)])

@@ -6,20 +6,24 @@ NL = NT + W
 NC = NL + P
 OFF = 2064.0
 KB = OFF - 7.5
+ZN, ZH = 1040, 528
+GROUPS = ((0, 2), (2, 4), (4, 7))
+PLAN = (0, 0, 1, 2, 3, 4, 5, 7)
+CUT = 640
 
 SCRATCH = {
     "lnI": ("sbuf", [128, 128], "int32"), "dsI": ("sbuf", [128, 128], "int32"),
-    "lnF": ("sbuf", [128, 128], "float16"), "dd": ("sbuf", [128, 128], "float16"),
+    "lnF": ("sbuf", [128, 128], "float16"), "dsF": ("sbuf", [128, 128], "float16"), "cum": ("sbuf", [128, 144], "float16"),
     "pI": ("sbuf", [128, 8], "int32"), "rtI": ("sbuf", [128, 8], "int32"), "qgI": ("sbuf", [128, 8], "int32"),
     "rt": ("sbuf", [128, 8], "float32"), "qg": ("sbuf", [128, 8], "float32"),
     "kb": ("sbuf", [128, 8], "float32"), "kc": ("sbuf", [128, 8], "float32"),
-    "selV": ("sbuf", [128, 128], "float32"), "Sel": ("sbuf", [128, 128], "float16"),
-    "rV": ("sbuf", [128, 128], "float32"), "mask": ("sbuf", [128, 256], "bfloat16"),
-    "bV": ("sbuf", [128, 8], "float32"), "B": ("sbuf", [128, 16], "float16"),
+    "selV": ("sbuf", [128, 128], "float32"), "Sel": ("sbuf", [128, 128], "float16"), "SelN": ("sbuf", [128, 128], "float16"),
+    "rV": ("sbuf", [128, 128], "float32"), "mask": ("sbuf", [128, 128], "bfloat16"),
+    "bV": ("sbuf", [128, 8], "float32"), "B": ("sbuf", [128, 8], "float16"),
     "qV": ("sbuf", [128, 144], "float32"), "Q": ("sbuf", [128, 144], "bfloat16"),
     "mV": ("sbuf", [128, NL], "float32"),
-    "Z": ("sbuf", [128, 1040], "float32"), "Zv": ("sbuf", [128, 128], "float32"), "ini": ("sbuf", [128, 8], "float32"),
-    "AA": ("sbuf", [128, 256], "float16"), "offs": ("sbuf", [128, 8], "uint16"),
+    "Z": ("sbuf", [128, ZN], "float32"), "Zv": ("sbuf", [128, 128], "float32"), "ini": ("sbuf", [128, 8], "float32"),
+    "AA": ("sbuf", [128, 128], "float16"), "offs": ("sbuf", [128, 8], "uint16"),
     "T0": ("sbuf", [128, NC], "bfloat16"), "T1": ("sbuf", [128, NC], "bfloat16"), "T2": ("sbuf", [128, NC], "bfloat16"),
     "L0": ("sbuf", [128, 64], "uint16"), "L1": ("sbuf", [128, 64], "uint16"), "L2": ("sbuf", [128, 64], "uint16"),
     "LF": ("sbuf", [128, 64], "uint16"),
@@ -28,6 +32,7 @@ SCRATCH = {
     "Y": ("sbuf", [128, P], "bfloat16"),
     "psA": ("psum", [128, 512], "float32"), "psE": ("psum", [128, 512], "float32"), "psD": ("psum", [128, 512], "float32"),
     "psW0": ("psum", [128, 512], "float32"), "psW1": ("psum", [128, 512], "float32"), "psW2": ("psum", [128, 512], "float32"),
+    "psW3": ("psum", [128, 512], "float32"),
 }
 SEMAPHORES = ["qv", "qa", "qp", "qg", "ldln", "ldds", "ldle", "st0", "st1", "lea", "sent"] + ["m%d" % s for s in range(8)]
 
@@ -155,38 +160,40 @@ def rank_program(g, core, T, topo):
     def fill(name, lo, hi, c):
         op("v", lambda q: q.memset(T[name][:, lo:hi], c), [], [(name, lo, hi)])
 
-    fill("mask", 0, 128, 1.0)
     vs(T.rtI[:, 0:1], T.pI[:, 0:1], 15, None, A.bitwise_and, None, [("pI", 0, 1)], [("rtI", 0, 1)])
     vs(T.qgI[:, 0:1], T.pI[:, 0:1], 4, None, A.arith_shift_right, None, [("pI", 0, 1)], [("qgI", 0, 1)])
-    vs(T.Sel[0:8, :], T.selV[0:8, :], 0.0, None, A.is_equal, None, [("selV", 0, 128)], [("Sel", 0, 128)])
     op("v", lambda q: q.tensor_copy(T.rt[:, 0:1], T.rtI[:, 0:1]), [("rtI", 0, 1)], [("rt", 0, 1)])
     op("v", lambda q: q.tensor_copy(T.qg[:, 0:1], T.qgI[:, 0:1]), [("qgI", 0, 1)], [("qg", 0, 1)])
-    vs(T.kc[:, 0:1], T.rtI[:, 0:1], KB + NL - 1, None, A.add, None, [("rtI", 0, 1)], [("kc", 0, 1)])
-    vs(T.kb[:, 0:1], T.rtI[:, 0:1], KB, None, A.add, None, [("rtI", 0, 1)], [("kb", 0, 1)])
-    vs(T.mask[:, 128:256], T.rV[:], T.rt[:, 0:1], None, A.is_ge, None, [("rV", 0, 128), ("rt", 0, 1)], [("mask", 128, 256)])
-    vs(T.B[:, 0:8], T.bV[:], T.qg[:, 0:1], None, A.is_gt, None, [("bV", 0, 8), ("qg", 0, 1)], [("B", 0, 8)])
-    vs(T.B[:, 8:16], T.bV[:], T.qg[:, 0:1], None, A.is_equal, None, [("bV", 0, 8), ("qg", 0, 1)], [("B", 8, 16)])
-    fill("Z", 0, 1040, 0.5)
+    for name, c in (("kc", KB + NL - 1), ("kb", KB)):
+        op("a", lambda q: q.activation(T[name][:, 0:1], T.rt[:, 0:1], F.Copy, bias=c), [("rt", 0, 1)], [(name, 0, 1)])
+    fill("Z", 0, ZH, 1.0)
+    op("a", lambda q: q.activation(T.Z[:, ZH:ZN], T.Z[:, 0:ZN - ZH], F.Copy), [("Z", 0, ZN - ZH)], [("Z", ZH, ZN)])
+    vs(T.Sel[0:8, :], T.selV[0:8, :], 0.0, None, A.is_equal, None, [("selV", 0, 128)], [("Sel", 0, 128)])
+    vs(T.SelN[0:8, :], T.selV[0:8, :], 0.0, -1.0, A.is_equal, A.mult, [("selV", 0, 128)], [("SelN", 0, 128)])
+    vs(T.cum[0:8, 0:16], T.selV[0:8, 0:16], 0.0, None, A.mult, None, [("selV", 0, 128)], [("cum", 0, 16)])
+    vs(T.mask[:], T.rV[:], T.rt[:, 0:1], None, A.is_ge, None, [("rV", 0, 128), ("rt", 0, 1)], [("mask", 0, 128)])
+    vs(T.B[:], T.bV[:], T.qg[:, 0:1], None, A.is_equal, None, [("bV", 0, 8), ("qg", 0, 1)], [("B", 0, 8)])
 
     vs(T.lnF[0:8, :], T.lnI[0:8, :], 1.0, None, A.add, None, [("lnI", 0, 128)], [("lnF", 0, 128)])
+    op("p", lambda q: q.matmul(T.psA[:, 0:128], T.lnF[0:8, :], T.Sel[0:8, :], True, True),
+       [("lnF", 0, 128), ("Sel", 0, 128)], [("psA", 0, 512)])
+    op("v", lambda q: q.tensor_copy(T.dsF[0:8, :], T.dsI[0:8, :]), [("dsI", 0, 128)], [("dsF", 0, 128)])
 
-    def mm_a(q):
-        q.matmul(T.psA[:, 0:128], T.lnF[0:8, :], T.Sel[0:8, :], True, True)
-        return q.matmul(T.psA[:, 128:256], T.lnF[0:8, :], T.Sel[0:8, :], True, True)
-    op("p", mm_a, [("lnF", 0, 128), ("Sel", 0, 128)], [("psA", 0, 512)])
-    op("v", lambda q: q.tensor_tensor(T.dd[0:8, 0:127], T.dsI[0:8, 0:127], T.dsI[0:8, 1:128], A.subtract),
-       [("dsI", 0, 128)], [("dd", 0, 127)])
-    op("v", lambda q: q.tensor_copy(T.dd[0:8, 127:128], T.dsI[0:8, 0:1]), [("dsI", 0, 128)], [("dd", 127, 128)])
-    op("p", lambda q: q.matmul(T.psD[:, 0:128], T.Sel[0:8, :], T.dd[0:8, :], True, True),
-       [("Sel", 0, 128), ("dd", 0, 128)], [("psD", 0, 512)])
-    op("v", lambda q: q.tensor_tensor(T.AA[:], T.psA[:, 0:256], T.mask[:], A.mult),
-       [("psA", 0, 512), ("mask", 0, 256)], [("AA", 0, 256)])
+    def mm_d(q):
+        q.matmul(T.psD[:, 0:127], T.Sel[0:8, :], T.dsF[0:8, 0:127], True, False)
+        q.matmul(T.psD[:, 0:127], T.SelN[0:8, :], T.dsF[0:8, 1:128], False, True)
+        return q.matmul(T.psD[:, 127:128], T.Sel[0:8, :], T.dsF[0:8, 0:1], True, True)
+    op("p", mm_d, [("Sel", 0, 128), ("SelN", 0, 128), ("dsF", 0, 128)], [("psD", 0, 512)])
+    op("v", lambda q: q.tensor_tensor_scan(T.cum[0:8, 16:144], T.lnF[0:8, :], T.lnF[0:8, :], 0.0, A.add, A.max),
+       [("lnF", 0, 128)], [("cum", 16, 144)])
+    op("v", lambda q: q.tensor_tensor(T.AA[:], T.psA[:, 0:128], T.mask[:], A.mult),
+       [("psA", 0, 512), ("mask", 0, 128)], [("AA", 0, 128)])
 
     def mm_e(q):
-        q.matmul(T.psE[:, 0:8], T.AA[:, 0:128], T.B[:, 0:8], True, False)
-        return q.matmul(T.psE[:, 0:8], T.AA[:, 128:256], T.B[:, 8:16], False, True)
-    op("p", mm_e, [("AA", 0, 256), ("B", 0, 16)], [("psE", 0, 512)])
-    op("a", lambda q: q.activation(T.Zv[:], T.psD[:, 0:128], F.Copy, bias=0.5, scale=0.5), [("psD", 0, 512)], [("Zv", 0, 128)])
+        q.matmul(T.psE[:, 0:8], T.Sel[0:8, :], T.cum[0:8, 15:128:16], True, False)
+        return q.matmul(T.psE[:, 0:8], T.AA[:], T.B[:], False, True)
+    op("p", mm_e, [("AA", 0, 128), ("B", 0, 8), ("cum", 0, 144), ("Sel", 0, 128)], [("psE", 0, 512)])
+    op("a", lambda q: q.activation(T.Zv[:], T.psD[:, 0:128], F.Copy, bias=1.0), [("psD", 0, 512)], [("Zv", 0, 128)])
     op("a", lambda q: q.activation(T.ini[:, 0:1], T.psD[:, 127:128], F.Identity, bias=T.kc[:, 0:1], scale=-1.0),
        [("psD", 0, 512), ("kc", 0, 1)], [("ini", 0, 1)])
     for b in range(3):
@@ -198,18 +205,19 @@ def rank_program(g, core, T, topo):
 
     op("v", lambda q: q.tensor_copy(T.Z[:, 8:8 + P].indirect(T.offs[:, 0:8]), T.Zv[:]),
        [("Zv", 0, 128), ("offs", 0, 8)], [("Z", 8, 8 + P)])
-    op("v", lambda q: q.tensor_tensor_scan(T.T0[:, NL:NC], T.Z[:, 7:7 + P], T.Z[:, 7:7 + P], T.ini[:, 0:1], A.add, A.add),
-       [("Z", 0, 1040), ("ini", 0, 1)], [("T0", NL, NC)])
+    op("v", lambda q: q.tensor_tensor_scan(T.T0[:, NL:NC], T.Z[:, 7:7 + P], T.Z[:, 7:7 + P], T.ini[:, 0:1], A.add, A.max),
+       [("Z", 0, ZN), ("ini", 0, 1)], [("T0", NL, NC)])
     op("v", lambda q: q.tensor_copy(T.T0[:, NL:NC].indirect(T.offs[:, 0:8]), T.T0[:, 0:NT]),
        [("T0", 0, NT), ("offs", 0, 8)], [("T0", NL, NC)])
 
     send(later, "D", NL * rank, NL * rank + NT, "lea", "D", NL * rank, NL * rank + NT)
 
-    def bank(n, hi):
-        return "psW%d" % (n % 3 if hi == P else (n + 1) % 3)
+    wrapped, nbank = {}, [0]
 
     def wrap(n, lo, hi):
-        tab, b = "T%d" % (n % 3), bank(n, hi)
+        tab, b = "T%d" % (n % 3), "psW%d" % (nbank[0] % 4)
+        nbank[0] += 1
+        wrapped[n, lo, hi] = b
 
         def go(q):
             for k in range(16):
@@ -217,9 +225,10 @@ def rank_program(g, core, T, topo):
             return last
         op("p", go, [("Q", 0, 144), (tab, NL + lo, NL + hi)], [(b, 0, 512)])
 
-    def to_list(n, name, lo, hi, c0):
-        b, w = bank(n, hi), (hi - lo) // 16
-        vs(T[name][:, c0:c0 + w], T[b][:, 0:w], -OFF, None, A.add, None, [(b, 0, 512)], [(name, c0, c0 + w)])
+    def to_list(n, name, lo, hi):
+        if (n, lo, hi) in wrapped:
+            b, c0, c1 = wrapped.pop((n, lo, hi)), lo // 16, hi // 16
+            vs(T[name][:, c0:c1], T[b][:, 0:c1 - c0], -OFF, None, A.add, None, [(b, 0, 512)], [(name, c0, c1)])
 
     def gather(e, out, olo, win, wlo, whi, lst, c0, c1):
         o, i = T[out][:, olo:olo + 16 * (c1 - c0)], T[win][:, wlo:whi].indirect(T[lst][:, c0:c1])
@@ -229,42 +238,41 @@ def rank_program(g, core, T, topo):
         else:
             op("a", lambda q: q.activation(o, i, F.Copy), r, w)
 
-    def compose(n, m, lo, hi):
-        new, old, lst = "T%d" % (n % 3), "T%d" % ((n - 1) % 3), "L%d" % (m % 3)
-        mid = (lo + hi) // 2
-        gather("v", new, NL + lo, old, 0, NC, lst, lo // 16, mid // 16)
-        gather("a", new, NL + mid, old, 0, NC, lst, mid // 16, hi // 16)
+    def both(out, olo, win, wlo, whi, lst, c0, c1):
+        mid = (c0 + c1) // 2
+        gather("v", out, olo, win, wlo, whi, lst, c0, mid)
+        gather("a", out, olo + 16 * (mid - c0), win, wlo, whi, lst, mid, c1)
 
+    def compose(n, lo, hi):
+        m = PLAN[n - 1]
+        to_list(m, "L%d" % (m % 3), lo, hi)
+        both("T%d" % (n % 3), NL + lo, "T%d" % ((n - 1) % 3), 0, NC, "L%d" % (m % 3), lo // 16, hi // 16)
+
+    last = len(PLAN)
     wrap(0, 0, P)
     fill("D", NT, NL, 0.0)
-    to_list(0, "L0", 0, P, 0)
-    compose(1, 0, 0, P)
-    wrap(1, 0, P)
-    for n in range(2, 9):
-        compose(n, n - 2, 0, P)
-        to_list(n - 1, "L%d" % ((n - 1) % 3), 0, P, 0)
-        if n < 8:
+    for n in range(1, last - 1):
+        compose(n, 0, P)
+        if n in PLAN:
             wrap(n, 0, P)
-    compose(9, 7, W, P)
-    wrap(9, W, P)
-    compose(9, 7, 0, W)
-    wrap(9, 0, W)
-    to_list(9, "LF", W, P, 32)
+    to_list(PLAN[last - 2], "L%d" % (PLAN[last - 2] % 3), 0, P)
+    for n in (last - 1, last):
+        for lo, hi in ((W, P), (0, W)):
+            compose(n, lo, hi)
+            wrap(n, lo, hi)
+    to_list(last, "LF", W, P)
     order = sorted(later, key=lambda c: -T.rank_of(c))
-    for a, b in ((0, 2), (2, 4), (4, 7)):
+    for a, b in GROUPS:
         send(order[a:b], "LF", 32, 64, "m%d" % rank, "M", 32 * rank, 32 * rank + 32)
-    to_list(9, "LF", 0, W, 0)
+    to_list(last, "LF", 0, W)
 
     for s in range(rank):
-        gather("v", "D", NL * (s + 1) + NT, "D", NL * s, NL * s + NL, "M", 32 * s, 32 * s + 16)
-        gather("a", "D", NL * (s + 1) + NT + 256, "D", NL * s, NL * s + NL, "M", 32 * s + 16, 32 * s + 32)
-    gather("v", "Y", 0, "D", NL * rank, NL * rank + NL, "LF", 0, 32)
-    gather("a", "Y", W, "D", NL * rank, NL * rank + NL, "LF", 32, 64)
-    dma("s", "st0", T.y[:, 0:W], T.Y[:, 0:W], [("Y", 0, W)], [])
-    dma("a", "st1", T.y[:, W:P], T.Y[:, W:P], [("Y", W, P)], [])
+        both("D", NL * (s + 1) + NT, "D", NL * s, NL * s + NL, "M", 32 * s, 32 * s + 32)
+    for h, (lo, hi) in enumerate(((0, CUT), (CUT, P))):
+        both("Y", lo, "D", NL * rank, NL * rank + NL, "LF", lo // 16, hi // 16)
+        dma("s", "st%d" % h, T.y[:, lo:hi], T.Y[:, lo:hi], [("Y", lo, hi)], [])
     for s in ("qv", "qa", "qp", "qg", "ldln", "ldds", "ldle"):
         await_tokens("s", [(s, count[s])])
     if sent[0]:
         g.wait_ge(T.sem.sent, sent[0])
-    await_tokens("s", [("st0", 16)])
-    await_tokens("a", [("st1", 16)])
+    await_tokens("s", [("st0", 16), ("st1", 16)])

@@ -4,27 +4,30 @@ from concourse.mybir import AluOpType, ActivationFunctionType
 P, NT, W = 1024, 128, 512
 NL = NT + W
 NC = NL + P
-OFF = 2064.0
-KB = OFF - 7.5
-ZN, ZH = 1040, 528
+HALF = 256
 GROUPS = ((0, 2), (2, 4), (4, 7))
 PLAN = (0, 0, 1, 2, 3, 4, 5, 7)
 CUT = 640
+NZ = 10
 
 SCRATCH = {
     "lnI": ("sbuf", [128, 128], "int32"), "dsI": ("sbuf", [128, 128], "int32"),
-    "lnF": ("sbuf", [128, 128], "float16"), "dsF": ("sbuf", [128, 128], "float16"), "cum": ("sbuf", [128, 144], "float16"),
-    "pI": ("sbuf", [128, 8], "int32"), "rtI": ("sbuf", [128, 8], "int32"), "qgI": ("sbuf", [128, 8], "int32"),
-    "rt": ("sbuf", [128, 8], "float32"), "qg": ("sbuf", [128, 8], "float32"),
-    "kb": ("sbuf", [128, 8], "float32"), "kc": ("sbuf", [128, 8], "float32"),
-    "selV": ("sbuf", [128, 128], "float32"), "Sel": ("sbuf", [128, 128], "float16"), "SelN": ("sbuf", [128, 128], "float16"),
-    "rV": ("sbuf", [128, 128], "float32"), "mask": ("sbuf", [128, 128], "bfloat16"),
-    "bV": ("sbuf", [128, 8], "float32"), "B": ("sbuf", [128, 8], "float16"),
-    "qV": ("sbuf", [128, 144], "float32"), "Q": ("sbuf", [128, 144], "bfloat16"),
-    "mV": ("sbuf", [128, NL], "float32"),
-    "Z": ("sbuf", [128, ZN], "float32"), "Zv": ("sbuf", [128, 128], "float32"), "ini": ("sbuf", [128, 8], "float32"),
-    "AA": ("sbuf", [128, 128], "float16"), "offs": ("sbuf", [128, 8], "uint16"),
-    "T0": ("sbuf", [128, NC], "bfloat16"), "T1": ("sbuf", [128, NC], "bfloat16"), "T2": ("sbuf", [128, NC], "bfloat16"),
+    "lnF": ("sbuf", [128, 128], "float16"), "cum": ("sbuf", [128, 144], "float16"), "X": ("sbuf", [128, 144], "float16"),
+    "pI": ("sbuf", [128, 8], "int32"), "k7I": ("sbuf", [128, 8], "int32"), "rtI": ("sbuf", [128, 8], "int32"),
+    "qgI": ("sbuf", [128, 8], "int32"),
+    "hN": ("sbuf", [128, 8], "float32"), "lN": ("sbuf", [128, 8], "float32"), "s2": ("sbuf", [128, 8], "float32"),
+    "w1": ("sbuf", [128, 8], "float32"), "w": ("sbuf", [128, 8], "float32"), "wN": ("sbuf", [128, 8], "float32"),
+    "lowX": ("sbuf", [128, 8], "float32"), "topX": ("sbuf", [128, 8], "float32"), "bias": ("sbuf", [128, 8], "float32"),
+    "qg": ("sbuf", [128, 8], "float32"), "rt": ("sbuf", [128, 8], "float32"), "pF": ("sbuf", [128, 8], "float32"),
+    "hs": ("sbuf", [128, 16], "float32"),
+    "x1": ("sbuf", [128, 128], "float32"), "c16": ("sbuf", [128, 128], "float32"), "r16": ("sbuf", [128, 128], "float32"),
+    "Sel": ("sbuf", [128, 128], "float16"), "mask": ("sbuf", [128, 128], "bfloat16"), "B": ("sbuf", [128, 8], "float16"),
+    "AA": ("sbuf", [128, 128], "float16"),
+    "wV": ("sbuf", [128, 144], "float32"), "WP": ("sbuf", [128, 144], "float16"), "WM": ("sbuf", [128, 144], "float16"),
+    "qV": ("sbuf", [128, 144], "float32"), "qU": ("sbuf", [128, 144], "float32"), "Q": ("sbuf", [128, 144], "bfloat16"),
+    "tmp": ("sbuf", [128, 144], "bfloat16"), "offs": ("sbuf", [128, 8], "uint16"),
+    "Z": ("sbuf", [128, NC], "bfloat16"),
+    "T0": ("sbuf", [128, NC], "bfloat16"), "T1": ("sbuf", [128, NC], "bfloat16"),
     "L0": ("sbuf", [128, 64], "uint16"), "L1": ("sbuf", [128, 64], "uint16"), "L2": ("sbuf", [128, 64], "uint16"),
     "LF": ("sbuf", [128, 64], "uint16"),
     "M": ("sbuf", [128, 256], "uint16"),
@@ -34,7 +37,7 @@ SCRATCH = {
     "psW0": ("psum", [128, 512], "float32"), "psW1": ("psum", [128, 512], "float32"), "psW2": ("psum", [128, 512], "float32"),
     "psW3": ("psum", [128, 512], "float32"),
 }
-SEMAPHORES = ["qv", "qa", "qp", "qg", "ldln", "ldds", "ldle", "st0", "st1", "lea", "sent"] + ["m%d" % s for s in range(8)]
+SEMAPHORES = ["qv", "qa", "qp", "qg", "ldln", "ldd0", "ldd1", "ldle", "st0", "st1", "lea", "sent"] + ["m%d" % s for s in range(8)]
 
 
 def rank_program(g, core, T, topo):
@@ -134,7 +137,8 @@ def rank_program(g, core, T, topo):
             record(None, ("m%d" % s, len(lanes(T.cores[s], core))), [], [("M", 32 * s, 32 * s + 32)])
 
     dma("s", "ldln", T.lnI[0:8, :], T.ln[:], [], [("lnI", 0, 128)])
-    dma("a", "ldds", T.dsI[0:8, :], T.ds[:], [], [("dsI", 0, 128)])
+    dma("a", "ldd0", T.dsI[0:8, :], T.ds[:], [], [("dsI", 0, 64)])
+    dma("s", "ldd1", T.dsI[8:16, :], T.ds[:], [], [("dsI", 64, 128)])
     dma("s", "ldle", T.D[:, NL * rank:NL * rank + NT], T.le[:], [], [("D", NL * rank, NL * rank + NT)])
 
     def iota(name, rows, n, pattern, base, cm):
@@ -144,12 +148,12 @@ def rank_program(g, core, T, topo):
         else:
             op("g", lambda q: q.iota(out, pattern, base, cm, allow_small_or_imprecise_dtypes=True), [], [(name, 0, n)])
 
-    iota("pI", 128, 1, [[1, 1]], 0, 1)
-    iota("selV", 8, 128, [[1, 8], [0, 16]], 0, -1)
-    iota("rV", 128, 128, [[0, 8], [1, 16]], 0, 0)
-    iota("bV", 128, 8, [[1, 8]], 0, 0)
+    iota("pI", 128, 2, [[0, 2]], 0, 1)
+    iota("c16", 128, 128, [[1, 8], [0, 16]], 0, 0)
+    iota("x1", 128, 128, [[1, 128]], 0, 0)
+    iota("r16", 128, 128, [[0, 8], [1, 16]], 0, 0)
+    iota("wV", 16, 144, [[1, 9], [8, 2], [100, 8]], -100, -1)
     iota("qV", 128, 144, [[1, 9], [1000, 16]], -1, 0)
-    iota("mV", 128, NL, [[1, NL]], 0, 0)
 
     def vs(out, in0, s1, s2, op0, op1, reads, writes):
         if op1 is None:
@@ -157,65 +161,93 @@ def rank_program(g, core, T, topo):
         else:
             op("v", lambda q: q.tensor_scalar(out, in0, s1, s2, op0, op1), reads, writes)
 
-    def fill(name, lo, hi, c):
-        op("v", lambda q: q.memset(T[name][:, lo:hi], c), [], [(name, lo, hi)])
+    def act(out, in_, func, reads, writes, bias=0.0, scale=1.0):
+        op("a", lambda q: q.activation(out, in_, func, bias=bias, scale=scale), reads, writes)
 
-    vs(T.rtI[:, 0:1], T.pI[:, 0:1], 15, None, A.bitwise_and, None, [("pI", 0, 1)], [("rtI", 0, 1)])
-    vs(T.qgI[:, 0:1], T.pI[:, 0:1], 4, None, A.arith_shift_right, None, [("pI", 0, 1)], [("qgI", 0, 1)])
-    op("v", lambda q: q.tensor_copy(T.rt[:, 0:1], T.rtI[:, 0:1]), [("rtI", 0, 1)], [("rt", 0, 1)])
-    op("v", lambda q: q.tensor_copy(T.qg[:, 0:1], T.qgI[:, 0:1]), [("qgI", 0, 1)], [("qg", 0, 1)])
-    for name, c in (("kc", KB + NL - 1), ("kb", KB)):
-        op("a", lambda q: q.activation(T[name][:, 0:1], T.rt[:, 0:1], F.Copy, bias=c), [("rt", 0, 1)], [(name, 0, 1)])
-    fill("Z", 0, ZH, 1.0)
-    op("a", lambda q: q.activation(T.Z[:, ZH:ZN], T.Z[:, 0:ZN - ZH], F.Copy), [("Z", 0, ZN - ZH)], [("Z", ZH, ZN)])
-    vs(T.Sel[0:8, :], T.selV[0:8, :], 0.0, None, A.is_equal, None, [("selV", 0, 128)], [("Sel", 0, 128)])
-    vs(T.SelN[0:8, :], T.selV[0:8, :], 0.0, -1.0, A.is_equal, A.mult, [("selV", 0, 128)], [("SelN", 0, 128)])
-    vs(T.cum[0:8, 0:16], T.selV[0:8, 0:16], 0.0, None, A.mult, None, [("selV", 0, 128)], [("cum", 0, 16)])
-    vs(T.mask[:], T.rV[:], T.rt[:, 0:1], None, A.is_ge, None, [("rV", 0, 128), ("rt", 0, 1)], [("mask", 0, 128)])
-    vs(T.B[:], T.bV[:], T.qg[:, 0:1], None, A.is_equal, None, [("bV", 0, 8), ("qg", 0, 1)], [("B", 0, 8)])
+    def col(name):
+        return T[name][:, 0:1]
+
+    def one(name):
+        return (name, 0, 1)
+
+    def copy_col(name, src):
+        op("v", lambda q: q.tensor_copy(col(name), col(src)), [one(src)], [one(name)])
+
+    vs(col("k7I"), col("pI"), 7, None, A.bitwise_and, None, [one("pI")], [one("k7I")])
+    vs(col("rtI"), col("pI"), 15, None, A.bitwise_and, None, [one("pI")], [one("rtI")])
+    vs(col("qgI"), col("pI"), 4, None, A.arith_shift_right, None, [one("pI")], [one("qgI")])
+    vs(T.lowX[0:16, 0:2], T.pI[0:16, 0:2], 8.0, float(HALF), A.is_lt, A.mult, [("pI", 0, 2)], [("lowX", 0, 2)])
+    copy_col("pF", "pI")
+    act(T.topX[0:16, 0:1], T.lowX[0:16, 0:1], F.Copy, [one("lowX")], [one("topX")], bias=float(HALF))
+    vs(col("hN"), col("k7I"), 2.0, -1.0, A.is_equal, A.mult, [one("k7I")], [one("hN")])
+    vs(col("lN"), col("k7I"), 3.0, -1.0, A.is_equal, A.mult, [one("k7I")], [one("lN")])
+    vs(col("s2"), col("k7I"), 2.0, None, A.is_lt, None, [one("k7I")], [one("s2")])
+    op("v", lambda q: q.tensor_copy(T.X[0:16, 0:130:129], T.lowX[0:16, 0:2]), [("lowX", 0, 2)], [("X", 0, 1), ("X", 129, 130)])
+    copy_col("rt", "rtI")
+    copy_col("qg", "qgI")
+    vs(T.Sel[0:8, :], T.c16[0:8, :], T.pF[0:8, 0:1], None, A.is_equal, None, [("c16", 0, 128), one("pF")], [("Sel", 0, 128)])
+    vs(T.B[:], T.c16[:, 0:128:16], col("qg"), None, A.is_equal, None, [("c16", 0, 128), one("qg")], [("B", 0, 8)])
+    vs(col("bias"), col("rtI"), 1.0, float(HALF), A.is_equal, A.mult, [one("rtI")], [one("bias")])
+    vs(T.mask[:], T.r16[:], col("rt"), None, A.is_ge, None, [("r16", 0, 128), one("rt")], [("mask", 0, 128)])
 
     vs(T.lnF[0:8, :], T.lnI[0:8, :], 1.0, None, A.add, None, [("lnI", 0, 128)], [("lnF", 0, 128)])
     op("p", lambda q: q.matmul(T.psA[:, 0:128], T.lnF[0:8, :], T.Sel[0:8, :], True, True),
        [("lnF", 0, 128), ("Sel", 0, 128)], [("psA", 0, 512)])
-    op("v", lambda q: q.tensor_copy(T.dsF[0:8, :], T.dsI[0:8, :]), [("dsI", 0, 128)], [("dsF", 0, 128)])
-
-    def mm_d(q):
-        q.matmul(T.psD[:, 0:127], T.Sel[0:8, :], T.dsF[0:8, 0:127], True, False)
-        q.matmul(T.psD[:, 0:127], T.SelN[0:8, :], T.dsF[0:8, 1:128], False, True)
-        return q.matmul(T.psD[:, 127:128], T.Sel[0:8, :], T.dsF[0:8, 0:1], True, True)
-    op("p", mm_d, [("Sel", 0, 128), ("SelN", 0, 128), ("dsF", 0, 128)], [("psD", 0, 512)])
+    vs(T.X[0:16, 1:129], T.dsI[0:16, :], T.lowX[0:16, 0:1], T.topX[0:16, 0:1], A.max, A.min,
+       [("dsI", 0, 128), one("lowX"), one("topX")], [("X", 1, 129)])
+    for name, c in (("WP", 1.0), ("WM", -1.0)):
+        vs(T[name][0:16, :], T.wV[0:16, :], 0.0, c, A.is_equal, A.mult, [("wV", 0, 144)], [(name, 0, 144)])
     op("v", lambda q: q.tensor_tensor_scan(T.cum[0:8, 16:144], T.lnF[0:8, :], T.lnF[0:8, :], 0.0, A.add, A.max),
        [("lnF", 0, 128)], [("cum", 16, 144)])
     op("v", lambda q: q.tensor_tensor(T.AA[:], T.psA[:, 0:128], T.mask[:], A.mult),
        [("psA", 0, 512), ("mask", 0, 128)], [("AA", 0, 128)])
 
-    def mm_e(q):
-        q.matmul(T.psE[:, 0:8], T.Sel[0:8, :], T.cum[0:8, 15:128:16], True, False)
-        return q.matmul(T.psE[:, 0:8], T.AA[:], T.B[:], False, True)
-    op("p", mm_e, [("AA", 0, 128), ("B", 0, 8), ("cum", 0, 144), ("Sel", 0, 128)], [("psE", 0, 512)])
-    op("a", lambda q: q.activation(T.Zv[:], T.psD[:, 0:128], F.Copy, bias=1.0), [("psD", 0, 512)], [("Zv", 0, 128)])
-    op("a", lambda q: q.activation(T.ini[:, 0:1], T.psD[:, 127:128], F.Identity, bias=T.kc[:, 0:1], scale=-1.0),
-       [("psD", 0, 512), ("kc", 0, 1)], [("ini", 0, 1)])
-    for b in range(3):
-        tab = T["T%d" % b]
-        op("a", lambda q: q.activation(tab[:, 0:NL], T.mV[:], F.Identity, bias=T.kb[:, 0:1]),
-           [("mV", 0, NL), ("kb", 0, 1)], [("T%d" % b, 0, NL)])
-    vs(T.Q[:], T.qV[:], T.qg[:, 0:1], 0.0625, A.is_equal, A.mult, [("qV", 0, 144), ("qg", 0, 1)], [("Q", 0, 144)])
-    vs(T.offs[:], T.psE[:, 0:8], -1.0, None, A.add, None, [("psE", 0, 512)], [("offs", 0, 8)])
+    act(col("w1"), col("hN"), F.Identity, [one("hN"), one("s2")], [one("w1")], bias=col("s2"), scale=-64.0)
+    act(T.hs[:, 0:13], T.x1[:, 0:13], F.Copy, [("x1", 0, 13), one("hN")], [("hs", 0, 13)], scale=col("hN"))
+    act(T.Z[:, 0:128], T.x1[:], F.Copy, [("x1", 0, 128), one("lN")], [("Z", 0, 128)], scale=col("lN"))
+    act(col("w"), col("lN"), F.Identity, [one("lN"), one("w1")], [one("w")], bias=col("w1"), scale=-0.5)
 
-    op("v", lambda q: q.tensor_copy(T.Z[:, 8:8 + P].indirect(T.offs[:, 0:8]), T.Zv[:]),
-       [("Zv", 0, 128), ("offs", 0, 8)], [("Z", 8, 8 + P)])
-    op("v", lambda q: q.tensor_tensor_scan(T.T0[:, NL:NC], T.Z[:, 7:7 + P], T.Z[:, 7:7 + P], T.ini[:, 0:1], A.add, A.max),
-       [("Z", 0, ZN), ("ini", 0, 1)], [("T0", NL, NC)])
-    op("v", lambda q: q.tensor_copy(T.T0[:, NL:NC].indirect(T.offs[:, 0:8]), T.T0[:, 0:NT]),
-       [("T0", 0, NT), ("offs", 0, 8)], [("T0", NL, NC)])
+    def block(e, n):
+        out, r, w = T.Z[:, 128 * n:128 * n + 128], [("Z", 0, 128), ("hs", n, n + 1)], [("Z", 128 * n, 128 * n + 128)]
+        if e == "v":
+            vs(out, T.Z[:, 0:128], T.hs[:, n:n + 1], None, A.add, None, r, w)
+        else:
+            act(out, T.Z[:, 0:128], F.Identity, r, w, bias=T.hs[:, n:n + 1])
+
+    for n in range(1, NZ):
+        block("a", n)
+
+    def mm_d(q):
+        q.matmul(T.psD[:, 0:129], T.WP[0:16, 1:129], T.X[0:16, 1:130], True, False)
+        q.matmul(T.psD[:, 0:129], T.WM[0:16, 1:129], T.X[0:16, 0:129], False, False)
+        return q.matmul(T.psD[:, 0:129], T.WM[0:16, 0:128], T.X[0:16, 1:130], False, True)
+    op("p", mm_d, [("WP", 0, 144), ("WM", 0, 144), ("X", 0, 130)], [("psD", 0, 512)])
+
+    def mm_e(q):
+        q.matmul(T.psE[:, 0:8], T.AA[:], T.B[:], True, False)
+        return q.matmul(T.psE[:, 1:8], T.Sel[0:8, :], T.cum[0:8, 31:128:16], False, True)
+    op("p", mm_e, [("AA", 0, 128), ("B", 0, 8), ("cum", 16, 144), ("Sel", 0, 128)], [("psE", 0, 512)])
+    act(T.tmp[:, 0:129], T.psD[:, 0:129], F.Identity, [("psD", 0, 512), one("bias")], [("tmp", 0, 129)], bias=col("bias"))
+
+    act(col("wN"), col("w"), F.Copy, [one("w")], [one("wN")], scale=-1.0)
+    act(T.qU[:], T.qV[:], F.Abs, [("qV", 0, 144), one("qg")], [("qU", 0, 144)], bias=col("qg"), scale=-1.0)
+    act(T.T0[:, 0:NL], T.Z[:, 0:NL], F.Copy, [("Z", 0, NL)], [("T0", 0, NL)])
+    act(T.Q[:], T.qU[:], F.Relu, [("qU", 0, 144), one("w"), one("wN")], [("Q", 0, 144)], bias=col("w"), scale=col("wN"))
+    for n in range(NZ, NC // 128):
+        block("v", n)
+
+    vs(T.offs[:], T.psE[:, 0:8], -1.0, None, A.add, None, [("psE", 0, 512)], [("offs", 0, 8)])
+    op("v", lambda q: q.tensor_tensor(T.Z[:, NL:NC].indirect(T.offs[:, 0:8]), T.tmp[:, 1:129], T.Z[:, 0:NT], A.add),
+       [("tmp", 1, 129), ("Z", 0, NT), ("offs", 0, 8)], [("Z", NL, NC)])
+    op("v", lambda q: q.tensor_tensor_scan(T.T0[:, NL:NC], T.Z[:, NL:NC], T.Z[:, NL:NC], T.tmp[:, 0:1], A.add, A.max),
+       [("Z", NL, NC), ("tmp", 0, 1)], [("T0", NL, NC)])
 
     send(later, "D", NL * rank, NL * rank + NT, "lea", "D", NL * rank, NL * rank + NT)
 
     wrapped, nbank = {}, [0]
 
     def wrap(n, lo, hi):
-        tab, b = "T%d" % (n % 3), "psW%d" % (nbank[0] % 4)
+        tab, b = "T%d" % (n % 2), "psW%d" % (nbank[0] % 4)
         nbank[0] += 1
         wrapped[n, lo, hi] = b
 
@@ -228,7 +260,7 @@ def rank_program(g, core, T, topo):
     def to_list(n, name, lo, hi):
         if (n, lo, hi) in wrapped:
             b, c0, c1 = wrapped.pop((n, lo, hi)), lo // 16, hi // 16
-            vs(T[name][:, c0:c1], T[b][:, 0:c1 - c0], -OFF, None, A.add, None, [(b, 0, 512)], [(name, c0, c1)])
+            vs(T[name][:, c0:c1], T[b][:, 0:c1 - c0], -1.0, None, A.mult, None, [(b, 0, 512)], [(name, c0, c1)])
 
     def gather(e, out, olo, win, wlo, whi, lst, c0, c1):
         o, i = T[out][:, olo:olo + 16 * (c1 - c0)], T[win][:, wlo:whi].indirect(T[lst][:, c0:c1])
@@ -246,16 +278,18 @@ def rank_program(g, core, T, topo):
     def compose(n, lo, hi):
         m = PLAN[n - 1]
         to_list(m, "L%d" % (m % 3), lo, hi)
-        both("T%d" % (n % 3), NL + lo, "T%d" % ((n - 1) % 3), 0, NC, "L%d" % (m % 3), lo // 16, hi // 16)
+        both("T%d" % (n % 2), NL + lo, "T%d" % ((n - 1) % 2), 0, NC, "L%d" % (m % 3), lo // 16, hi // 16)
 
     last = len(PLAN)
     wrap(0, 0, P)
-    fill("D", NT, NL, 0.0)
+    op("v", lambda q: q.memset(T.D[:, NT:NL], 0.0), [], [("D", NT, NL)])
+    op("v", lambda q: q.tensor_copy(T.T1[:, 0:NL], T.Z[:, 0:NL]), [("Z", 0, NL)], [("T1", 0, NL)])
     for n in range(1, last - 1):
         compose(n, 0, P)
         if n in PLAN:
             wrap(n, 0, P)
-    to_list(PLAN[last - 2], "L%d" % (PLAN[last - 2] % 3), 0, P)
+    m = PLAN[last - 2]
+    to_list(m, "L%d" % (m % 3), 0, P)
     for n in (last - 1, last):
         for lo, hi in ((W, P), (0, W)):
             compose(n, lo, hi)
@@ -271,7 +305,7 @@ def rank_program(g, core, T, topo):
     for h, (lo, hi) in enumerate(((0, CUT), (CUT, P))):
         both("Y", lo, "D", NL * rank, NL * rank + NL, "LF", lo // 16, hi // 16)
         dma("s", "st%d" % h, T.y[:, lo:hi], T.Y[:, lo:hi], [("Y", lo, hi)], [])
-    for s in ("qv", "qa", "qp", "qg", "ldln", "ldds", "ldle"):
+    for s in ("qv", "qa", "qp", "qg", "ldln", "ldd0", "ldd1", "ldle"):
         await_tokens("s", [(s, count[s])])
     if sent[0]:
         g.wait_ge(T.sem.sent, sent[0])

from concourse.bass import DstId, RemoteDMATransfer
from concourse.mybir import AluOpType, ActivationFunctionType

P, NT, W = 1024, 128, 512
NL = NT + W
NC = NL + P
HALF = 256
GROUPS = ((0, 2), (2, 4), (4, 7))
PLAN = (0, 0, 1, 2, 3, 4, 5, 7)
CUT = 640
NZ = 10

SCRATCH = {
    "lnI": ("sbuf", [128, 128], "int32"), "dsI": ("sbuf", [128, 128], "int32"),
    "lnF": ("sbuf", [128, 128], "float16"), "cum": ("sbuf", [128, 144], "float16"), "X": ("sbuf", [128, 144], "float16"),
    "pI": ("sbuf", [128, 8], "int32"), "k7I": ("sbuf", [128, 8], "int32"), "rtI": ("sbuf", [128, 8], "int32"),
    "qgI": ("sbuf", [128, 8], "int32"),
    "hN": ("sbuf", [128, 8], "float32"), "lN": ("sbuf", [128, 8], "float32"), "s2": ("sbuf", [128, 8], "float32"),
    "w1": ("sbuf", [128, 8], "float32"), "w": ("sbuf", [128, 8], "float32"), "wN": ("sbuf", [128, 8], "float32"),
    "lowX": ("sbuf", [128, 8], "float32"), "topX": ("sbuf", [128, 8], "float32"), "bias": ("sbuf", [128, 8], "float32"),
    "qg": ("sbuf", [128, 8], "float32"), "rt": ("sbuf", [128, 8], "float32"), "pF": ("sbuf", [128, 8], "float32"),
    "hs": ("sbuf", [128, 16], "float32"),
    "x1": ("sbuf", [128, 128], "float32"), "c16": ("sbuf", [128, 128], "float32"), "r16": ("sbuf", [128, 128], "float32"),
    "Sel": ("sbuf", [128, 128], "float16"), "mask": ("sbuf", [128, 128], "bfloat16"), "B": ("sbuf", [128, 8], "float16"),
    "AA": ("sbuf", [128, 128], "float16"),
    "wV": ("sbuf", [128, 144], "float32"), "WP": ("sbuf", [128, 144], "float16"), "WM": ("sbuf", [128, 144], "float16"),
    "qV": ("sbuf", [128, 144], "float32"), "qU": ("sbuf", [128, 144], "float32"), "Q": ("sbuf", [128, 144], "bfloat16"),
    "tmp": ("sbuf", [128, 144], "bfloat16"), "offs": ("sbuf", [128, 8], "uint16"),
    "Z": ("sbuf", [128, NC], "bfloat16"),
    "T0": ("sbuf", [128, NC], "bfloat16"), "T1": ("sbuf", [128, NC], "bfloat16"),
    "L0": ("sbuf", [128, 64], "uint16"), "L1": ("sbuf", [128, 64], "uint16"), "L2": ("sbuf", [128, 64], "uint16"),
    "LF": ("sbuf", [128, 64], "uint16"),
    "M": ("sbuf", [128, 256], "uint16"),
    "D": ("sbuf", [128, 8 * NL], "bfloat16"),
    "Y": ("sbuf", [128, P], "bfloat16"),
    "psA": ("psum", [128, 512], "float32"), "psE": ("psum", [128, 512], "float32"), "psD": ("psum", [128, 512], "float32"),
    "psW0": ("psum", [128, 512], "float32"), "psW1": ("psum", [128, 512], "float32"), "psW2": ("psum", [128, 512], "float32"),
    "psW3": ("psum", [128, 512], "float32"),
}
SEMAPHORES = ["qv", "qa", "qp", "qg", "ldln", "ldd0", "ldd1", "ldle", "st0", "st1", "lea", "sent"] + ["m%d" % s for s in range(8)]


def rank_program(g, core, T, topo):
    rank = T.rank_of(core)
    if rank is None:
        return
    queue = {"v": g.vector, "a": g.scalar, "p": g.tensor, "g": g, "s": g.sync}
    known = {e: {} for e in queue}
    snap = {}
    count = {}
    acc = {}

    def await_tokens(e, toks):
        best = {}
        for s, v in toks:
            if known[e].get(s, 0) < v:
                best[s] = max(best.get(s, 0), v)
        for s, v in sorted(best.items()):
            if any(t != s and snap.get((t, best[t]), {}).get(s, 0) >= v for t in best):
                continue
            if known[e].get(s, 0) >= v:
                continue
            queue[e].wait_ge(T.sem[s], v)
            known[e][s] = v
            for t, w in snap.get((s, v), {}).items():
                known[e][t] = max(known[e].get(t, 0), w)

    def depend(e, reads, writes):
        toks = []
        for b, lo, hi in reads:
            toks += [a[3] for a in acc.get(b, []) if a[2] and a[0] < hi and lo < a[1]]
        for b, lo, hi in writes:
            toks += [a[3] for a in acc.get(b, []) if a[0] < hi and lo < a[1]]
        await_tokens(e, toks)

    def record(e, tok, reads, writes):
        if e is not None:
            snap[tok] = dict(known[e])
            snap[tok][tok[0]] = tok[1]
        for b, lo, hi in writes:
            acc[b] = [a for a in acc.get(b, []) if not (lo <= a[0] and a[1] <= hi)] + [[lo, hi, True, tok]]
        for b, lo, hi in reads:
            acc.setdefault(b, []).append([lo, hi, False, tok])

    def op(e, call, reads, writes):
        depend(e, reads, writes)
        s = "q" + e
        count[s] = count.get(s, 0) + 1
        call(queue[e]).then_inc(T.sem[s], 1)
        record(e, (s, count[s]), reads, writes)

    def dma(e, sem, out, in_, reads, writes):
        depend(e, reads, writes)
        count[sem] = count.get(sem, 0) + 16
        queue[e].dma_start(out, in_).then_inc(T.sem[sem], 16)
        record(e, (sem, count[sem]), reads, writes)

    later = [c for c in T.cores if T.rank_of(c) > rank]
    sent = [0]

    def lanes(src, dst):
        if topo.chip(src) != topo.chip(dst):
            return topo.engines(src, dst)
        off = [x for c in T.cores if topo.chip(c) != topo.chip(src) and T.rank_of(c) > T.rank_of(src)
               for x in topo.engines(src, c)]
        return [x for x in topo.engines(src, dst) if x not in off]

    def send(cores, name, lo, hi, sem, dst_name, dlo, dhi):
        if not cores:
            return
        depend("g", [(name, lo, hi)], [])
        sets = []
        for c in cores:
            e = lanes(core, c)
            same = [x for x in sets if x[0] == e]
            if same:
                same[0][1].append(c)
            else:
                sets.append([e, [c]])
        trs = []
        for e, cs in sets:
            ids = []
            for c in cs:
                rid, pid, _ = topo.addr(c)
                ids.append(DstId(rid=rid, pnc=pid))
            trs.append(RemoteDMATransfer(dst_ids=ids, dma_engine_mask=sum(1 << x for x in e), remote_sem=T.sem[sem],
                                         srcs=[T[name][:, lo:hi]], dsts=[T[dst_name][:, dlo:dhi] for _ in cs]))
            sent[0] += len(e)
        g.remote_dma_fused(trs, local_sem=T.sem.sent)

    A, F = AluOpType, ActivationFunctionType

    if rank:
        record(None, ("lea", sum(len(lanes(T.cores[s], core)) for s in range(rank))), [],
               [("D", NL * s, NL * s + NT) for s in range(rank)])
        for s in range(rank):
            record(None, ("m%d" % s, len(lanes(T.cores[s], core))), [], [("M", 32 * s, 32 * s + 32)])

    dma("s", "ldln", T.lnI[0:8, :], T.ln[:], [], [("lnI", 0, 128)])
    dma("a", "ldd0", T.dsI[0:8, :], T.ds[:], [], [("dsI", 0, 64)])
    dma("s", "ldd1", T.dsI[8:16, :], T.ds[:], [], [("dsI", 64, 128)])
    dma("s", "ldle", T.D[:, NL * rank:NL * rank + NT], T.le[:], [], [("D", NL * rank, NL * rank + NT)])

    def iota(name, rows, n, pattern, base, cm):
        out = T[name][0:rows, 0:n]
        if name == "pI":
            op("g", lambda q: q.iota(out, pattern, base, cm), [], [(name, 0, n)])
        else:
            op("g", lambda q: q.iota(out, pattern, base, cm, allow_small_or_imprecise_dtypes=True), [], [(name, 0, n)])

    iota("pI", 128, 2, [[0, 2]], 0, 1)
    iota("c16", 128, 128, [[1, 8], [0, 16]], 0, 0)
    iota("x1", 128, 128, [[1, 128]], 0, 0)
    iota("r16", 128, 128, [[0, 8], [1, 16]], 0, 0)
    iota("wV", 16, 144, [[1, 9], [8, 2], [100, 8]], -100, -1)
    iota("qV", 128, 144, [[1, 9], [1000, 16]], -1, 0)

    def vs(out, in0, s1, s2, op0, op1, reads, writes):
        if op1 is None:
            op("v", lambda q: q.tensor_scalar(out, in0, s1, None, op0), reads, writes)
        else:
            op("v", lambda q: q.tensor_scalar(out, in0, s1, s2, op0, op1), reads, writes)

    def act(out, in_, func, reads, writes, bias=0.0, scale=1.0):
        op("a", lambda q: q.activation(out, in_, func, bias=bias, scale=scale), reads, writes)

    def col(name):
        return T[name][:, 0:1]

    def one(name):
        return (name, 0, 1)

    def copy_col(name, src):
        op("v", lambda q: q.tensor_copy(col(name), col(src)), [one(src)], [one(name)])

    vs(col("k7I"), col("pI"), 7, None, A.bitwise_and, None, [one("pI")], [one("k7I")])
    vs(col("rtI"), col("pI"), 15, None, A.bitwise_and, None, [one("pI")], [one("rtI")])
    vs(col("qgI"), col("pI"), 4, None, A.arith_shift_right, None, [one("pI")], [one("qgI")])
    vs(T.lowX[0:16, 0:2], T.pI[0:16, 0:2], 8.0, float(HALF), A.is_lt, A.mult, [("pI", 0, 2)], [("lowX", 0, 2)])
    copy_col("pF", "pI")
    act(T.topX[0:16, 0:1], T.lowX[0:16, 0:1], F.Copy, [one("lowX")], [one("topX")], bias=float(HALF))
    vs(col("hN"), col("k7I"), 2.0, -1.0, A.is_equal, A.mult, [one("k7I")], [one("hN")])
    vs(col("lN"), col("k7I"), 3.0, -1.0, A.is_equal, A.mult, [one("k7I")], [one("lN")])
    vs(col("s2"), col("k7I"), 2.0, None, A.is_lt, None, [one("k7I")], [one("s2")])
    op("v", lambda q: q.tensor_copy(T.X[0:16, 0:130:129], T.lowX[0:16, 0:2]), [("lowX", 0, 2)], [("X", 0, 1), ("X", 129, 130)])
    copy_col("rt", "rtI")
    copy_col("qg", "qgI")
    vs(T.Sel[0:8, :], T.c16[0:8, :], T.pF[0:8, 0:1], None, A.is_equal, None, [("c16", 0, 128), one("pF")], [("Sel", 0, 128)])
    vs(T.B[:], T.c16[:, 0:128:16], col("qg"), None, A.is_equal, None, [("c16", 0, 128), one("qg")], [("B", 0, 8)])
    vs(col("bias"), col("rtI"), 1.0, float(HALF), A.is_equal, A.mult, [one("rtI")], [one("bias")])
    vs(T.mask[:], T.r16[:], col("rt"), None, A.is_ge, None, [("r16", 0, 128), one("rt")], [("mask", 0, 128)])

    vs(T.lnF[0:8, :], T.lnI[0:8, :], 1.0, None, A.add, None, [("lnI", 0, 128)], [("lnF", 0, 128)])
    op("p", lambda q: q.matmul(T.psA[:, 0:128], T.lnF[0:8, :], T.Sel[0:8, :], True, True),
       [("lnF", 0, 128), ("Sel", 0, 128)], [("psA", 0, 512)])
    vs(T.X[0:16, 1:129], T.dsI[0:16, :], T.lowX[0:16, 0:1], T.topX[0:16, 0:1], A.max, A.min,
       [("dsI", 0, 128), one("lowX"), one("topX")], [("X", 1, 129)])
    for name, c in (("WP", 1.0), ("WM", -1.0)):
        vs(T[name][0:16, :], T.wV[0:16, :], 0.0, c, A.is_equal, A.mult, [("wV", 0, 144)], [(name, 0, 144)])
    op("v", lambda q: q.tensor_tensor_scan(T.cum[0:8, 16:144], T.lnF[0:8, :], T.lnF[0:8, :], 0.0, A.add, A.max),
       [("lnF", 0, 128)], [("cum", 16, 144)])
    op("v", lambda q: q.tensor_tensor(T.AA[:], T.psA[:, 0:128], T.mask[:], A.mult),
       [("psA", 0, 512), ("mask", 0, 128)], [("AA", 0, 128)])

    act(col("w1"), col("hN"), F.Identity, [one("hN"), one("s2")], [one("w1")], bias=col("s2"), scale=-64.0)
    act(T.hs[:, 0:13], T.x1[:, 0:13], F.Copy, [("x1", 0, 13), one("hN")], [("hs", 0, 13)], scale=col("hN"))
    act(T.Z[:, 0:128], T.x1[:], F.Copy, [("x1", 0, 128), one("lN")], [("Z", 0, 128)], scale=col("lN"))
    act(col("w"), col("lN"), F.Identity, [one("lN"), one("w1")], [one("w")], bias=col("w1"), scale=-0.5)

    def block(e, n):
        out, r, w = T.Z[:, 128 * n:128 * n + 128], [("Z", 0, 128), ("hs", n, n + 1)], [("Z", 128 * n, 128 * n + 128)]
        if e == "v":
            vs(out, T.Z[:, 0:128], T.hs[:, n:n + 1], None, A.add, None, r, w)
        else:
            act(out, T.Z[:, 0:128], F.Identity, r, w, bias=T.hs[:, n:n + 1])

    for n in range(1, NZ):
        block("a", n)

    def mm_d(q):
        q.matmul(T.psD[:, 0:129], T.WP[0:16, 1:129], T.X[0:16, 1:130], True, False)
        q.matmul(T.psD[:, 0:129], T.WM[0:16, 1:129], T.X[0:16, 0:129], False, False)
        return q.matmul(T.psD[:, 0:129], T.WM[0:16, 0:128], T.X[0:16, 1:130], False, True)
    op("p", mm_d, [("WP", 0, 144), ("WM", 0, 144), ("X", 0, 130)], [("psD", 0, 512)])

    def mm_e(q):
        q.matmul(T.psE[:, 0:8], T.AA[:], T.B[:], True, False)
        return q.matmul(T.psE[:, 1:8], T.Sel[0:8, :], T.cum[0:8, 31:128:16], False, True)
    op("p", mm_e, [("AA", 0, 128), ("B", 0, 8), ("cum", 16, 144), ("Sel", 0, 128)], [("psE", 0, 512)])
    act(T.tmp[:, 0:129], T.psD[:, 0:129], F.Identity, [("psD", 0, 512), one("bias")], [("tmp", 0, 129)], bias=col("bias"))

    act(col("wN"), col("w"), F.Copy, [one("w")], [one("wN")], scale=-1.0)
    act(T.qU[:], T.qV[:], F.Abs, [("qV", 0, 144), one("qg")], [("qU", 0, 144)], bias=col("qg"), scale=-1.0)
    act(T.T0[:, 0:NL], T.Z[:, 0:NL], F.Copy, [("Z", 0, NL)], [("T0", 0, NL)])
    act(T.Q[:], T.qU[:], F.Relu, [("qU", 0, 144), one("w"), one("wN")], [("Q", 0, 144)], bias=col("w"), scale=col("wN"))
    for n in range(NZ, NC // 128):
        block("v", n)

    vs(T.offs[:], T.psE[:, 0:8], -1.0, None, A.add, None, [("psE", 0, 512)], [("offs", 0, 8)])
    op("v", lambda q: q.tensor_tensor(T.Z[:, NL:NC].indirect(T.offs[:, 0:8]), T.tmp[:, 1:129], T.Z[:, 0:NT], A.add),
       [("tmp", 1, 129), ("Z", 0, NT), ("offs", 0, 8)], [("Z", NL, NC)])
    op("v", lambda q: q.tensor_tensor_scan(T.T0[:, NL:NC], T.Z[:, NL:NC], T.Z[:, NL:NC], T.tmp[:, 0:1], A.add, A.max),
       [("Z", NL, NC), ("tmp", 0, 1)], [("T0", NL, NC)])

    send(later, "D", NL * rank, NL * rank + NT, "lea", "D", NL * rank, NL * rank + NT)

    wrapped, nbank = {}, [0]

    def wrap(n, lo, hi):
        tab, b = "T%d" % (n % 2), "psW%d" % (nbank[0] % 4)
        nbank[0] += 1
        wrapped[n, lo, hi] = b

        def go(q):
            for k in range(16):
                last = q.matmul(T[b][:, 0:(hi - lo) // 16], T.Q[:, 16 - k:144 - k], T[tab][:, NL + lo + k:NL + hi:16], k == 0, k == 15)
            return last
        op("p", go, [("Q", 0, 144), (tab, NL + lo, NL + hi)], [(b, 0, 512)])

    def to_list(n, name, lo, hi):
        if (n, lo, hi) in wrapped:
            b, c0, c1 = wrapped.pop((n, lo, hi)), lo // 16, hi // 16
            vs(T[name][:, c0:c1], T[b][:, 0:c1 - c0], -1.0, None, A.mult, None, [(b, 0, 512)], [(name, c0, c1)])

    def gather(e, out, olo, win, wlo, whi, lst, c0, c1):
        o, i = T[out][:, olo:olo + 16 * (c1 - c0)], T[win][:, wlo:whi].indirect(T[lst][:, c0:c1])
        r, w = [(win, wlo, whi), (lst, c0, c1)], [(out, olo, olo + 16 * (c1 - c0))]
        if e == "v":
            op("v", lambda q: q.tensor_copy(o, i), r, w)
        else:
            op("a", lambda q: q.activation(o, i, F.Copy), r, w)

    def both(out, olo, win, wlo, whi, lst, c0, c1):
        mid = (c0 + c1) // 2
        gather("v", out, olo, win, wlo, whi, lst, c0, mid)
        gather("a", out, olo + 16 * (mid - c0), win, wlo, whi, lst, mid, c1)

    def compose(n, lo, hi):
        m = PLAN[n - 1]
        to_list(m, "L%d" % (m % 3), lo, hi)
        both("T%d" % (n % 2), NL + lo, "T%d" % ((n - 1) % 2), 0, NC, "L%d" % (m % 3), lo // 16, hi // 16)

    last = len(PLAN)
    wrap(0, 0, P)
    op("v", lambda q: q.memset(T.D[:, NT:NL], 0.0), [], [("D", NT, NL)])
    op("v", lambda q: q.tensor_copy(T.T1[:, 0:NL], T.Z[:, 0:NL]), [("Z", 0, NL)], [("T1", 0, NL)])
    for n in range(1, last - 1):
        compose(n, 0, P)
        if n in PLAN:
            wrap(n, 0, P)
    m = PLAN[last - 2]
    to_list(m, "L%d" % (m % 3), 0, P)
    for n in (last - 1, last):
        for lo, hi in ((W, P), (0, W)):
            compose(n, lo, hi)
            wrap(n, lo, hi)
    to_list(last, "LF", W, P)
    order = sorted(later, key=lambda c: -T.rank_of(c))
    for a, b in GROUPS:
        send(order[a:b], "LF", 32, 64, "m%d" % rank, "M", 32 * rank, 32 * rank + 32)
    to_list(last, "LF", 0, W)

    for s in range(rank):
        both("D", NL * (s + 1) + NT, "D", NL * s, NL * s + NL, "M", 32 * s, 32 * s + 32)
    for h, (lo, hi) in enumerate(((0, CUT), (CUT, P))):
        both("Y", lo, "D", NL * rank, NL * rank + NL, "LF", lo // 16, hi // 16)
        dma("s", "st%d" % h, T.y[:, lo:hi], T.Y[:, lo:hi], [("Y", lo, hi)], [])
    for s in ("qv", "qa", "qp", "qg", "ldln", "ldd0", "ldd1", "ldle"):
        await_tokens("s", [(s, count[s])])
    if sent[0]:
        g.wait_ge(T.sem.sent, sent[0])
    await_tokens("s", [("st0", 16), ("st1", 16)])
